import numpy as np
import ml_dtypes


def mxq(x, axis, fmt="e4m3"):
    dtype, down = {"e4m3": (ml_dtypes.float8_e4m3fn, 7), "e5m2": (ml_dtypes.float8_e5m2, 14)}[fmt]
    v = np.moveaxis(np.asarray(x, np.float32).astype(ml_dtypes.bfloat16).astype(np.float64), axis, -1)
    blocks = v.reshape(v.shape[:-1] + (-1, 32))
    amax = np.abs(blocks).max(-1, keepdims=True)
    byte = np.maximum(np.where(amax > 0, np.frexp(amax)[1] - 1 + 127, 0) - down, 1)
    scale = np.exp2(byte - 127.0)
    codes = (blocks / scale).astype(np.float32).astype(dtype).astype(np.float64)
    return np.moveaxis((codes * scale).reshape(v.shape), -1, axis)


WIDE = False


def mx_kscale(k):
    if not WIDE:
        return np.ones(k)
    levels = np.array([10, -10, 5, -5, 0])
    if k % 512:
        return np.exp2(np.random.permutation(np.resize(levels, k // 32))).repeat(32)
    a = np.empty((k // 512, 16))
    for p in range(k // 512):
        a[p, :8] = np.random.permutation(np.resize(levels, 8))
        for g in range(8):
            far = levels[np.abs(levels - a[p, g]) >= 10]
            a[p, g + 8] = far[np.random.randint(len(far))]
    return np.exp2(a.ravel()).repeat(32)


BF16 = ml_dtypes.bfloat16


def bf(x):
    return np.asarray(x, np.float32).astype(BF16)


def f64(x):
    return np.asarray(x).astype(np.float64)


T, D, H, N = 1024, 1024, 4, 32
TWO = 2
C = H * TWO * N
SLOTS = N * N


def draw0():
    s = mx_kscale(D)
    t = mx_kscale(SLOTS)
    return {
        "x": bf(np.random.standard_normal((T, D)) * s),
        "wk": bf(np.random.standard_normal((D, C)) * 1.5 / np.sqrt(D) / s[:, None]),
        "slot_gain": bf(np.random.standard_normal(SLOTS) * np.sqrt(SLOTS) * t),
        "values": bf(np.random.standard_normal((SLOTS, D)) * 2.0 / np.sqrt(SLOTS) / t[:, None]),
        "wg": bf(np.random.standard_normal((D, D)) * 1.5 / np.sqrt(D) / s[:, None]),
    }


def softmax(v):
    e = np.exp(v - v.max(-1, keepdims=True))
    return e / e.sum(-1, keepdims=True)


def product_key_weights(sc):
    p = softmax(sc)
    p1 = p[:, :, 0, :]
    p2 = p[:, :, 1, :]
    w = np.sum(p1[:, :, :, None] * p2[:, :, None, :], axis=1)
    return w.reshape(w.shape[0], SLOTS)


def core(x, wk, slot_gain, values, wg):
    xq = mxq(f64(x), 1, "e4m3")
    sc = (xq @ mxq(f64(wk), 0, "e4m3")).reshape(x.shape[0], H, TWO, N)
    w = product_key_weights(sc)
    wg_slots = w * f64(slot_gain)[None, :]
    mem = mxq(wg_slots, 1, "e4m3") @ mxq(f64(values), 0, "e4m3")
    a = xq @ mxq(f64(wg), 0, "e4m3")
    gate = a * (1.0 / (1.0 + np.exp(-a)))
    return mem * gate


def e4m3fn_bytes(y):
    return np.clip(np.asarray(y, np.float64), -448.0, 448.0).astype(np.float32).astype(ml_dtypes.float8_e4m3fn).view(np.uint8)


def e4m3fn_values(b):
    return np.asarray(b, np.uint8).view(ml_dtypes.float8_e4m3fn).astype(np.float64)


def setup_inputs():
    d = draw0()
    x0 = np.asarray(d['x']).astype(np.float64)
    s = (np.max(np.abs(x0), axis=(0,), keepdims=True) / 448.0).astype(np.float32)
    out = {}
    for k, v in d.items():
        if k == 'x':
            out['x_bytes'] = e4m3fn_bytes(x0 / s.astype(np.float64))
            out['x_scale'] = s
        else:
            out[k] = v
    return out


def reference(x_bytes, x_scale, wk, slot_gain, values, wg):
    return core(e4m3fn_values(x_bytes) * x_scale.astype(np.float64), wk, slot_gain, values, wg)

@@ -1,0 +1,370 @@
+from contextlib import ExitStack
+
+import concourse.mybir as mybir
+from concourse.masks import make_identity
+
+T, D, C, SLOTS = 1024, 1024, 256, 1024
+H, N = 4, 32
+P = 128
+G = 2
+TILES = T // P
+PAIRS = TILES // 2
+
+FLOPS = 2 * T * D * (C + D + D)
+
+F32 = mybir.dt.float32
+BF16 = mybir.dt.bfloat16
+U32 = mybir.dt.uint32
+U8 = mybir.dt.uint8
+FP8 = mybir.dt.float8_e4m3fn
+FP8X4 = mybir.dt.float8_e4m3fn_x4
+ACT = mybir.ActivationFunctionType
+ALU = mybir.AluOpType
+AX = mybir.AxisListType
+
+HEAD_ENGINE = "VVSG"
+WG_ENGINE = "SGSG"
+VAL_ENGINE = "GSVV"
+
+
+def tile_productkeysoftmemoryplus_kernel(tc, x_bytes, x_scale, wk, slot_gain, values, wg, out):
+    nc = tc.nc
+    with ExitStack() as ctx:
+        keep = ctx.enter_context(tc.tile_pool(name="keep", bufs=1))
+        work = ctx.enter_context(tc.tile_pool(name="work", bufs=2))
+        psum = ctx.enter_context(tc.psum_pool(name="psum", bufs=1))
+
+        ident = keep.tile([P, P], F32, name="ident")
+        xb = [keep.tile([P, 2, D], U8, name="xb%d" % q) for q in range(PAIRS)]
+        scale_t = keep.tile([P, G, 4], F32, name="scale_t")
+        gain_t = keep.tile([P, G, 4], BF16, name="gain_t")
+        wk_raw = keep.tile([P, G, 4, C], BF16, name="wk_raw")
+        wg_raw = [keep.tile([P, 4, D], BF16, name="wg_raw%d" % g) for g in range(G)]
+        val_raw = [keep.tile([P, 4, D], BF16, name="val_raw%d" % g) for g in range(G)]
+
+        def load_x(q):
+            nc.sync.dma_start(out=xb[q][:], in_=x_bytes[q * 256 : (q + 1) * 256, :].rearrange("(i p) d -> p i d", p=P))
+
+        load_x(0)
+        nc.sync.dma_start(out=scale_t[:], in_=x_scale.rearrange("o (g p t) -> p (o g) t", p=P, t=4))
+        nc.sync.dma_start(out=wk_raw[:], in_=wk.rearrange("(g p t) c -> p g t c", p=P, t=4))
+        load_x(1)
+        nc.sync.dma_start(out=gain_t[:], in_=slot_gain.rearrange("(g p t) -> p g t", p=P, t=4))
+        for g in range(G):
+            nc.sync.dma_start(out=wg_raw[g][:], in_=wg[g * 512 : (g + 1) * 512, :].rearrange("(p t) n -> p t n", t=4))
+        load_x(2)
+        load_x(3)
+        for g in range(G):
+            nc.sync.dma_start(out=val_raw[g][:], in_=values[g * 512 : (g + 1) * 512, :].rearrange("(p t) n -> p t n", t=4))
+
+        make_identity(nc, ident[:])
+
+        wk_i = keep.tile([P, G, C, 4], BF16, name="wk_i", align_bytes=64)
+        wk_c = keep.tile([P, G, C], U32, name="wk_c", align_bytes=64)
+        wk_s = keep.tile([P, G, C], U8, name="wk_s", align_bytes=64)
+
+        def prep_wk():
+            for g in range(G):
+                src = wk_raw[:, g].rearrange("p t (h a n) -> p t h a n", h=H, a=2)
+                nc.vector.tensor_copy(
+                    out=wk_i[:, g, 0:128, :].rearrange("p (h n) t -> p h n t", h=H),
+                    in_=src[:, :, :, 0, :].rearrange("p t h n -> p h n t"),
+                )
+                for h in range(H):
+                    nc.vector.tensor_copy(
+                        out=wk_i[:, g, 128 + 32 * h : 160 + 32 * h, :].rearrange("p (m j) t -> p m j t", m=4),
+                        in_=src[:, :, h, 1, :].rearrange("p t (j m) -> p m j t", m=4),
+                    )
+            nc.vector.quantize_mx(
+                out=wk_c[:].rearrange("p g c -> p (g c)").bitcast(FP8X4),
+                scales=wk_s[:].rearrange("p g c -> p (g c)"),
+                in_=wk_i[:].rearrange("p g c t -> p (g c t)"),
+            )
+
+        codes = {}
+        for nm in ("wg", "val"):
+            codes[nm] = (
+                [[keep.tile([P, 512], U32, name="%s_c%d%d" % (nm, g, nh), align_bytes=64) for nh in range(2)] for g in range(G)],
+                [[keep.tile([P, 512], U8, name="%s_s%d%d" % (nm, g, nh), align_bytes=64) for nh in range(2)] for g in range(G)],
+            )
+        staged = {}
+
+        def interleave_w(nm, raw, g, nh, eng):
+            st = work.tile([P, 512, 4], BF16, name="w_i", align_bytes=64, bufs=4)
+            src = raw[g][:, :, nh * 512 : (nh + 1) * 512].rearrange("p t n -> p n t")
+            if eng == "V":
+                nc.vector.tensor_copy(out=st[:], in_=src)
+            elif eng == "S":
+                nc.scalar.copy(out=st[:], in_=src)
+            else:
+                nc.gpsimd.tensor_scalar(out=st[:], in0=src, scalar1=1.0, scalar2=0.0, op0=ALU.mult, op1=ALU.add)
+            staged[nm, g, nh] = st
+
+        def quant_w(nm, g, nh):
+            nc.vector.quantize_mx(
+                out=codes[nm][0][g][nh][:].bitcast(FP8X4),
+                scales=codes[nm][1][g][nh][:],
+                in_=staged[nm, g, nh][:].rearrange("p n t -> p (n t)"),
+            )
+
+        xw, xt, xg = {}, {}, {}
+        xq_c = [keep.tile([P, 2, G, P], U32, name="xq_c%d" % q, align_bytes=64) for q in range(PAIRS)]
+        xq_s = [keep.tile([P, 2, G, P], U8, name="xq_s%d" % q, align_bytes=64) for q in range(PAIRS)]
+        uq_c = [keep.tile([P, G, P], U32, name="uq_c%d" % i, align_bytes=64) for i in range(TILES)]
+        uq_s = [keep.tile([P, G, P], U8, name="uq_s%d" % i, align_bytes=64) for i in range(TILES)]
+
+        def widen(q, eng):
+            xw[q] = work.tile([P, 2, D], BF16, name="xw", align_bytes=64)
+            src = xb[q][:].bitcast(FP8)
+            if eng == "S":
+                nc.scalar.copy(out=xw[q][:], in_=src)
+            elif eng == "V":
+                nc.vector.tensor_copy(out=xw[q][:], in_=src)
+            else:
+                nc.gpsimd.tensor_copy(out=xw[q][:], in_=src)
+
+        def x_transposes(q):
+            words = xw[q][:].rearrange("p i d -> p (i d)").bitcast(F32)
+            xt[q] = []
+            for i in range(2):
+                bank = psum.tile([P, G, 2, P], F32, name="mm", bufs=6)
+                for g in range(G):
+                    for u in range(2):
+                        w0 = i * 512 + g * 256 + u
+                        nc.tensor.transpose(bank[:, g, u, :], words[:, w0 : w0 + 255 : 2], ident[:])
+                xt[q].append(bank)
+
+        def x_empty(q):
+            xg[q] = work.tile([P, 2, G, P, 4], BF16, name="xg", align_bytes=64)
+            for i in range(2):
+                for g in range(G):
+                    nc.vector.tensor_tensor(
+                        out=xg[q][:, i, g].rearrange("p r (u e) -> p r u e", u=2),
+                        in0=xt[q][i][:, g].rearrange("p u r -> p (u r)").bitcast(BF16).rearrange("p (u r e) -> p r u e", u=2, e=2),
+                        in1=scale_t[:, g].rearrange("p (u e) -> p u e", u=2).unsqueeze(1).to_broadcast([P, P, 2, 2]),
+                        op=ALU.mult,
+                    )
+
+        def x_quant(q):
+            nc.vector.quantize_mx(
+                out=xq_c[q][:].rearrange("p i g r -> p (i g r)").bitcast(FP8X4),
+                scales=xq_s[q][:].rearrange("p i g r -> p (i g r)"),
+                in_=xg[q][:].rearrange("p i g r t -> p (i g r t)"),
+            )
+
+        scb, nmax, zs, et, p1n = {}, {}, {}, {}, {}
+
+        def scores(q):
+            scb[q] = psum.tile([P, 2, C], F32, name="mm", bufs=6)
+            for i in range(2):
+                for g in range(G):
+                    nc.tensor.matmul_mx(
+                        out=scb[q][:, i, :],
+                        lhsT=xq_c[q][:, i, g, :].bitcast(FP8X4),
+                        lhsT_scale=xq_s[q][:, i, g, :],
+                        rhs=wk_c[:, g, :].bitcast(FP8X4),
+                        rhs_scale=wk_s[:, g, :],
+                        start=(g == 0),
+                        stop=(g == G - 1),
+                    )
+
+        def soft_max(q):
+            mx = work.tile([P, 16], F32, name="mx")
+            nc.vector.tensor_reduce(out=mx[:], in_=scb[q][:].rearrange("p i (k n) -> p (i k) n", n=N), axis=AX.X, op=ALU.max)
+            nmax[q] = work.tile([P, 16], F32, name="nmax")
+            nc.vector.tensor_scalar(out=nmax[q][:], in0=mx[:], scalar1=-1.0, scalar2=None, op0=ALU.mult)
+
+        def soft_exp(q):
+            et[q] = work.tile([P, 2, 2, H, N], F32, name="et", bufs=4)
+            zs[q] = work.tile([P, 2, 2, H], F32, name="zs", bufs=4)
+            for i in range(2):
+                for a in range(2):
+                    for h in range(H):
+                        k = a * H + h
+                        nc.scalar.activation(
+                            out=et[q][:, i, a, h, :],
+                            in_=scb[q][:, i, k * N : (k + 1) * N],
+                            func=ACT.Exp,
+                            bias=nmax[q][:, i * 8 + k : i * 8 + k + 1],
+                            accum_out=zs[q][:, i, a, h : h + 1],
+                        )
+
+        def soft_norm(q):
+            zz = work.tile([P, 2, H], F32, name="zz")
+            nc.vector.tensor_tensor(out=zz[:], in0=zs[q][:, :, 0, :], in1=zs[q][:, :, 1, :], op=ALU.mult)
+            rz = work.tile([P, 2, H], F32, name="rz")
+            nc.vector.reciprocal(out=rz[:], in_=zz[:])
+            p1n[q] = work.tile([P, 2, H, N], F32, name="p1n", bufs=4)
+            for i in range(2):
+                nc.vector.tensor_tensor(
+                    out=p1n[q][:, i], in0=et[q][:, i, 0], in1=rz[:, i, :].unsqueeze(2).to_broadcast([P, H, N]), op=ALU.mult
+                )
+
+        prod = {}
+
+        def products(i, which):
+            q, j = i // 2, i % 2
+            for h in range(H):
+                e = HEAD_ENGINE[h]
+                if e != which:
+                    continue
+                pt = work.tile([P, 4, N, 8], F32, name="prod%d" % h, align_bytes=64)
+                prod[i, h] = pt
+                if e == "S":
+                    src = et[q][:, j, 1, h, :].rearrange("p (m j) -> p m j", m=4)
+                    for k in range(N):
+                        nc.scalar.activation(out=pt[:, :, k, :], in_=src, func=ACT.Copy, scale=p1n[q][:, j, h, k : k + 1])
+                else:
+                    eng = nc.vector if e == "V" else nc.gpsimd
+                    eng.tensor_tensor(
+                        out=pt[:],
+                        in0=p1n[q][:, j, h, :].unsqueeze(1).unsqueeze(3).to_broadcast([P, 4, N, 8]),
+                        in1=et[q][:, j, 1, h, :].rearrange("p (m j) -> p m j", m=4).unsqueeze(2).to_broadcast([P, 4, N, 8]),
+                        op=ALU.mult,
+                    )
+
+        ut, ug = {}, {}
+
+        def u_transposes(i):
+            ut[i] = []
+            for g in range(G):
+                bank = psum.tile([P, 4, P], F32, name="ut", bufs=2)
+                for m in range(4):
+                    for h in range(H):
+                        nc.tensor.matmul(
+                            out=bank[:, m, :],
+                            lhsT=prod[i, h][:, m, 16 * g : 16 * g + 16, :].rearrange("p i j -> p (i j)"),
+                            rhs=ident[:],
+                            is_transpose=True,
+                            start=(h == 0),
+                            stop=(h == H - 1),
+                        )
+                ut[i].append(bank)
+
+        def u_empty(i):
+            ug[i] = work.tile([P, G, P, 4], BF16, name="ug", align_bytes=64)
+            for g in range(G):
+                nc.vector.tensor_tensor(
+                    out=ug[i][:, g],
+                    in0=ut[i][g][:].rearrange("p m r -> p r m"),
+                    in1=gain_t[:, g].unsqueeze(1).to_broadcast([P, P, 4]),
+                    op=ALU.mult,
+                )
+
+        def u_quant(i):
+            nc.vector.quantize_mx(
+                out=uq_c[i][:].rearrange("p g r -> p (g r)").bitcast(FP8X4),
+                scales=uq_s[i][:].rearrange("p g r -> p (g r)"),
+                in_=ug[i][:].rearrange("p g r t -> p (g r t)"),
+            )
+
+        ab, mb, gate = {}, {}, {}
+
+        def mm(lc, ls, nm, nh):
+            bank = psum.tile([P, 512], F32, name="mm", bufs=6)
+            for g in range(G):
+                nc.tensor.matmul_mx(
+                    out=bank[:],
+                    lhsT=lc[g].bitcast(FP8X4),
+                    lhsT_scale=ls[g],
+                    rhs=codes[nm][0][g][nh][:].bitcast(FP8X4),
+                    rhs_scale=codes[nm][1][g][nh][:],
+                    start=(g == 0),
+                    stop=(g == G - 1),
+                )
+            return bank
+
+        def a_mm(i):
+            q, j = i // 2, i % 2
+            for nh in range(2):
+                ab[i, nh] = mm([xq_c[q][:, j, g, :] for g in range(G)], [xq_s[q][:, j, g, :] for g in range(G)], "wg", nh)
+
+        def m_mm(i):
+            for nh in range(2):
+                mb[i, nh] = mm([uq_c[i][:, g, :] for g in range(G)], [uq_s[i][:, g, :] for g in range(G)], "val", nh)
+
+        def silu(i):
+            gate[i] = work.tile([P, 2, 512], F32, name="gate")
+            for nh in range(2):
+                nc.scalar.activation(out=gate[i][:, nh, :], in_=ab[i, nh][:], func=ACT.Silu)
+
+        def final(i):
+            o = work.tile([P, 2, 512], F32, name="o", bufs=3)
+            for nh in range(2):
+                nc.vector.tensor_tensor(out=o[:, nh, :], in0=mb[i, nh][:], in1=gate[i][:, nh, :], op=ALU.mult)
+            nc.sync.dma_start(out=out[i * P : (i + 1) * P, :], in_=o[:].rearrange("p a n -> p (a n)"))
+
+        def front(q):
+            x_transposes(q)
+            x_empty(q)
+            x_quant(q)
+            scores(q)
+            soft_max(q)
+            soft_exp(q)
+            soft_norm(q)
+
+        def prods(i):
+            products(i, "S")
+            products(i, "G")
+            products(i, "V")
+
+        def mid(i):
+            u_transposes(i)
+            u_empty(i)
+            u_quant(i)
+
+        def back(i):
+            a_mm(i)
+            silu(i)
+            m_mm(i)
+            final(i)
+
+        wjobs = [("wg", wg_raw, g, nh, WG_ENGINE[2 * g + nh]) for g in range(G) for nh in range(2)]
+        wjobs += [("val", val_raw, g, nh, VAL_ENGINE[2 * g + nh]) for g in range(G) for nh in range(2)]
+
+        def wprep(j):
+            nm, raw, g, nh, eng = wjobs[j]
+            interleave_w(nm, raw, g, nh, eng)
+            quant_w(nm, g, nh)
+
+        widen(0, "S")
+        prep_wk()
+        front(0)
+        widen(1, "G")
+        wprep(0)
+        wprep(1)
+        prods(0)
+        front(1)
+        widen(2, "G")
+        mid(0)
+        prods(1)
+        wprep(2)
+        wprep(3)
+        front(2)
+        widen(3, "G")
+        mid(1)
+        prods(2)
+        wprep(4)
+        wprep(5)
+        front(3)
+        mid(2)
+        prods(3)
+        wprep(6)
+        wprep(7)
+        back(0)
+        mid(3)
+        prods(4)
+        back(1)
+        back(2)
+        mid(4)
+        prods(5)
+        back(3)
+        mid(5)
+        prods(6)
+        back(4)
+        mid(6)
+        prods(7)
+        back(5)
+        mid(7)
+        back(6)
+        back(7)

@@ -22,9 +22,29 @@ ACT = mybir.ActivationFunctionType
 ALU = mybir.AluOpType
 AX = mybir.AxisListType
 
-HEAD_ENGINE = "VVSG"
-WG_ENGINE = "SGSG"
-VAL_ENGINE = "GSVV"
+PLAN = """ WD:0:V XT:0 WK WD:1:S XT:1 WKQ XE:0 WI:0:G:384:512 WD:2:S WI:0:G:256:384 XE:1 WD:3:S XT:2 WI:0:G:128:256 XQ:0
+ XT:3 XE:2 WI:0:G:0:128 WD:4:S WI:1:G:384:512 XE:3 WI:1:G:256:384 WD:5:S XT:4 SC:0 XQ:1 XE:4 WI:1:G:128:256
+ WD:6:S XT:5 WI:1:G:0:128 SC:1 MX:0 WD:7:S XQ:2 XE:5 EX:0 MX:1 WI:2:V:256:512 WI:3:S:256:512 PT:0 XT:6 NZ:0
+ SC:2 NR:0 WI:2:V:0:256 EX:1 NM:0 XQ:3 PR:0:0:3:G XE:6 WI:3:S:0:256 PT:1 XT:7 SC:3 MX:2 WI:4:S:256:512 NZ:1
+ XQ:4 NR:1 MX:3 SC:4 XQ:5 NM:1 PC:1 XQ:6 PC:0 PB:1 WI:4:S:0:256 PR:1:0:0:G MX:4 PB:0 PR:1:0:1:V PR:1:0:3:V
+ PR:1:0:2:G EX:2 PR:1:1:1:V PR:0:0:0:V WI:5:S:256:512 PT:2 PR:1:1:0:G PR:0:0:1:V PR:0:0:2:V PC:2 WI:6:S:256:512
+ PR:1:1:2:G PR:0:1:0:V UT:0:0 PR:0:1:1:V PR:0:1:2:V PR:1:1:3:G WI:5:S:0:256 PR:0:1:3:V UT:0:1 NZ:2 XE:7
+ WI:7:G:384:512 EX:3 WI:7:G:256:384 WI:6:S:0:256 NR:2 PB:2 SC:5 XQ:7 PT:3 UE:0:0 WI:7:G:128:256 PC:3 UE:0:1
+ PB:3 UT:1:0 MX:5 NZ:3 NM:2 PR:2:0:0:S PR:2:0:1:G PR:2:0:2:V SC:6 UT:1:1 PR:2:0:3:V PR:2:1:1:S PR:2:1:2:G
+ PR:2:1:0:V PR:2:1:3:S UE:1:0 SC:7 WI:7:G:0:128 MX:6 UE:1:1 EX:4 WQ:1 PT:4 WQ:2 UT:2:0 PC:4 EX:5 WQ:0 MX:7 EX:6
+ A:0:0 WQ:3 NZ:4 PB:4 NR:3 WQ:4 EX:7 UT:2:1 WQ:5 SL:0:0 NZ:5 NM:3 A:1:0 PR:3:0:1:G PR:3:0:0:V A:0:1 PR:3:0:2:V
+ A:2:0 PR:3:0:3:G PR:3:1:1:V SL:0:1 PR:3:1:2:V A:1:1 SL:1:0 PR:3:1:0:G PR:3:1:3:V A:3:0 SL:1:1 UE:2:0 A:2:1
+ SL:2:0 WQ:6 UT:3:0 SL:3:0 UE:2:1 SL:2:1 NZ:6 NZ:7 WQ:7 UT:3:1 NR:4 UQ:0 NM:4 PR:4:0:0:G PR:4:0:3:S PR:4:0:2:V
+ MM:0:0 PR:4:1:0:V PR:4:1:1:S MM:0:1 PR:4:0:1:G PR:4:1:3:V A:4:0 PR:4:1:2:S FN:0:0 A:3:1 FN:0:1 A:4:1 SL:4:0
+ UQ:1 A:5:0 UE:3:0 SL:3:1 MM:1:0 UE:3:1 SL:4:1 MM:1:1 FN:1:0 UT:4:0 NR:5 SL:5:0 NM:5 UQ:2 PR:5:0:0:S PR:5:0:1:G
+ FN:1:1 UT:4:1 PR:5:0:3:S UQ:3 PR:5:0:2:G NR:6 PR:5:1:1:S MM:2:0 MM:2:1 PR:5:1:2:S NM:6 PR:5:1:0:G FN:2:0 A:5:1
+ NR:7 A:6:0 SL:5:1 NM:7 MM:3:0 PR:5:1:3:G FN:2:1 SL:6:0 MM:3:1 UE:4:0 PR:6:0:1:S A:6:1 UE:4:1 PR:6:0:0:G
+ PR:6:0:3:S UT:5:0 UQ:4 PR:6:1:0:S PR:6:0:2:G FN:3:0 UT:5:1 FN:3:1 PR:6:1:2:S UE:5:0 PR:6:1:1:G PR:6:1:3:S
+ A:7:0 UE:5:1 MM:4:0 PR:7:0:0:G SL:6:1 MM:4:1 PR:7:0:1:S A:7:1 UQ:5 PR:7:0:3:G FN:4:0 UT:6:0 PR:7:0:2:S FN:4:1
+ PR:7:1:1:S PR:7:1:0:G UT:6:1 UE:6:0 PR:7:1:3:S PR:7:1:2:G SL:7:0 MM:5:0 UE:6:1 SL:7:1 MM:5:1 UQ:6 UT:7:0
+ FN:5:0 FN:5:1 UT:7:1 UE:7:0 MM:6:0 UE:7:1 MM:6:1 UQ:7 FN:6:0 MM:7:0 FN:6:1 MM:7:1 FN:7:0 FN:7:1"""
+P2 = True
+II = False
 
 
 def tile_productkeysoftmemoryplus_kernel(tc, x_bytes, x_scale, wk, slot_gain, values, wg, out):
@@ -35,27 +55,36 @@ def tile_productkeysoftmemoryplus_kernel(tc, x_bytes, x_scale, wk, slot_gain, va
         psum = ctx.enter_context(tc.psum_pool(name="psum", bufs=1))
 
         ident = keep.tile([P, P], F32, name="ident")
-        xb = [keep.tile([P, 2, D], U8, name="xb%d" % q) for q in range(PAIRS)]
+        xb = [keep.tile([P, D], U8, name="xb%d" % i) for i in range(TILES)]
         scale_t = keep.tile([P, G, 4], F32, name="scale_t")
+        scale_b = keep.tile([P, D], F32, name="scale_b")
         gain_t = keep.tile([P, G, 4], BF16, name="gain_t")
         wk_raw = keep.tile([P, G, 4, C], BF16, name="wk_raw")
         wg_raw = [keep.tile([P, 4, D], BF16, name="wg_raw%d" % g) for g in range(G)]
         val_raw = [keep.tile([P, 4, D], BF16, name="val_raw%d" % g) for g in range(G)]
 
-        def load_x(q):
-            nc.sync.dma_start(out=xb[q][:], in_=x_bytes[q * 256 : (q + 1) * 256, :].rearrange("(i p) d -> p i d", p=P))
+        def load_x(i):
+            nc.sync.dma_start(out=xb[i][:], in_=x_bytes[i * P : (i + 1) * P, :])
+
+        def load_w(dst, src, g):
+            nc.sync.dma_start(out=dst[g][:], in_=src[g * 512 : (g + 1) * 512, :].rearrange("(p t) n -> p t n", t=4))
 
         load_x(0)
-        nc.sync.dma_start(out=scale_t[:], in_=x_scale.rearrange("o (g p t) -> p (o g) t", p=P, t=4))
+        if II:
+            nc.sync.dma_start(out=scale_b[:], in_=x_scale.rearrange("o k -> (o k)").partition_broadcast(P))
+        else:
+            nc.sync.dma_start(out=scale_t[:], in_=x_scale.rearrange("o (g p t) -> p (o g) t", p=P, t=4))
         nc.sync.dma_start(out=wk_raw[:], in_=wk.rearrange("(g p t) c -> p g t c", p=P, t=4))
         load_x(1)
+        load_w(wg_raw, wg, 0)
         nc.sync.dma_start(out=gain_t[:], in_=slot_gain.rearrange("(g p t) -> p g t", p=P, t=4))
-        for g in range(G):
-            nc.sync.dma_start(out=wg_raw[g][:], in_=wg[g * 512 : (g + 1) * 512, :].rearrange("(p t) n -> p t n", t=4))
         load_x(2)
         load_x(3)
-        for g in range(G):
-            nc.sync.dma_start(out=val_raw[g][:], in_=values[g * 512 : (g + 1) * 512, :].rearrange("(p t) n -> p t n", t=4))
+        load_w(wg_raw, wg, 1)
+        for i in range(4, TILES):
+            load_x(i)
+        load_w(val_raw, values, 0)
+        load_w(val_raw, values, 1)
 
         make_identity(nc, ident[:])
 
@@ -63,7 +92,7 @@ def tile_productkeysoftmemoryplus_kernel(tc, x_bytes, x_scale, wk, slot_gain, va
         wk_c = keep.tile([P, G, C], U32, name="wk_c", align_bytes=64)
         wk_s = keep.tile([P, G, C], U8, name="wk_s", align_bytes=64)
 
-        def prep_wk():
+        def prep_wk_i():
             for g in range(G):
                 src = wk_raw[:, g].rearrange("p t (h a n) -> p t h a n", h=H, a=2)
                 nc.vector.tensor_copy(
@@ -75,6 +104,8 @@ def tile_productkeysoftmemoryplus_kernel(tc, x_bytes, x_scale, wk, slot_gain, va
                         out=wk_i[:, g, 128 + 32 * h : 160 + 32 * h, :].rearrange("p (m j) t -> p m j t", m=4),
                         in_=src[:, :, h, 1, :].rearrange("p t (j m) -> p m j t", m=4),
                     )
+
+        def prep_wk_q():
             nc.vector.quantize_mx(
                 out=wk_c[:].rearrange("p g c -> p (g c)").bitcast(FP8X4),
                 scales=wk_s[:].rearrange("p g c -> p (g c)"),
@@ -89,184 +120,195 @@ def tile_productkeysoftmemoryplus_kernel(tc, x_bytes, x_scale, wk, slot_gain, va
             )
         staged = {}
 
-        def interleave_w(nm, raw, g, nh, eng):
-            st = work.tile([P, 512, 4], BF16, name="w_i", align_bytes=64, bufs=4)
-            src = raw[g][:, :, nh * 512 : (nh + 1) * 512].rearrange("p t n -> p n t")
+        def wi(j, eng, c0, c1):
+            nm, raw, g, nh = (("wg", wg_raw), ("val", val_raw))[j // 4] + ((j // 2) % 2, j % 2)
+            if j not in staged:
+                staged[j] = work.tile([P, 512, 4], BF16, name="w_i", align_bytes=64, bufs=8)
+            st = staged[j][:, c0:c1, :]
+            src = raw[g][:, :, nh * 512 + c0 : nh * 512 + c1].rearrange("p t n -> p n t")
             if eng == "V":
-                nc.vector.tensor_copy(out=st[:], in_=src)
+                nc.vector.tensor_copy(out=st, in_=src)
             elif eng == "S":
-                nc.scalar.copy(out=st[:], in_=src)
+                nc.scalar.copy(out=st, in_=src)
             else:
-                nc.gpsimd.tensor_scalar(out=st[:], in0=src, scalar1=1.0, scalar2=0.0, op0=ALU.mult, op1=ALU.add)
-            staged[nm, g, nh] = st
+                nc.gpsimd.tensor_scalar(out=st, in0=src, scalar1=1.0, scalar2=0.0, op0=ALU.mult, op1=ALU.add)
 
-        def quant_w(nm, g, nh):
+        def wq(j):
+            nm, g, nh = ("wg", "val")[j // 4], (j // 2) % 2, j % 2
             nc.vector.quantize_mx(
                 out=codes[nm][0][g][nh][:].bitcast(FP8X4),
                 scales=codes[nm][1][g][nh][:],
-                in_=staged[nm, g, nh][:].rearrange("p n t -> p (n t)"),
+                in_=staged[j][:].rearrange("p n t -> p (n t)"),
             )
 
         xw, xt, xg = {}, {}, {}
-        xq_c = [keep.tile([P, 2, G, P], U32, name="xq_c%d" % q, align_bytes=64) for q in range(PAIRS)]
-        xq_s = [keep.tile([P, 2, G, P], U8, name="xq_s%d" % q, align_bytes=64) for q in range(PAIRS)]
+        xq_c = [keep.tile([P, G, P], U32, name="xq_c%d" % i, align_bytes=64) for i in range(TILES)]
+        xq_s = [keep.tile([P, G, P], U8, name="xq_s%d" % i, align_bytes=64) for i in range(TILES)]
         uq_c = [keep.tile([P, G, P], U32, name="uq_c%d" % i, align_bytes=64) for i in range(TILES)]
         uq_s = [keep.tile([P, G, P], U8, name="uq_s%d" % i, align_bytes=64) for i in range(TILES)]
 
-        def widen(q, eng):
-            xw[q] = work.tile([P, 2, D], BF16, name="xw", align_bytes=64)
-            src = xb[q][:].bitcast(FP8)
-            if eng == "S":
-                nc.scalar.copy(out=xw[q][:], in_=src)
-            elif eng == "V":
-                nc.vector.tensor_copy(out=xw[q][:], in_=src)
+        def widen(i, e):
+            xw[i] = work.tile([P, D], BF16, name="xw", align_bytes=64, bufs=3)
+            src = xb[i][:].bitcast(FP8)
+            if e == "S":
+                nc.scalar.copy(out=xw[i][:], in_=src)
+            elif e == "V":
+                nc.vector.tensor_copy(out=xw[i][:], in_=src)
             else:
-                nc.gpsimd.tensor_copy(out=xw[q][:], in_=src)
+                nc.gpsimd.tensor_copy(out=xw[i][:], in_=src)
 
-        def x_transposes(q):
-            words = xw[q][:].rearrange("p i d -> p (i d)").bitcast(F32)
-            xt[q] = []
-            for i in range(2):
-                bank = psum.tile([P, G, 2, P], F32, name="mm", bufs=6)
-                for g in range(G):
-                    for u in range(2):
-                        w0 = i * 512 + g * 256 + u
-                        nc.tensor.transpose(bank[:, g, u, :], words[:, w0 : w0 + 255 : 2], ident[:])
-                xt[q].append(bank)
+        def x_scale_product(i):
+            xw[i] = work.tile([P, D], BF16, name="xw", align_bytes=64, bufs=3)
+            nc.vector.tensor_tensor(out=xw[i][:], in0=xb[i][:].bitcast(FP8), in1=scale_b[:], op=ALU.mult)
 
-        def x_empty(q):
-            xg[q] = work.tile([P, 2, G, P, 4], BF16, name="xg", align_bytes=64)
-            for i in range(2):
-                for g in range(G):
-                    nc.vector.tensor_tensor(
-                        out=xg[q][:, i, g].rearrange("p r (u e) -> p r u e", u=2),
-                        in0=xt[q][i][:, g].rearrange("p u r -> p (u r)").bitcast(BF16).rearrange("p (u r e) -> p r u e", u=2, e=2),
-                        in1=scale_t[:, g].rearrange("p (u e) -> p u e", u=2).unsqueeze(1).to_broadcast([P, P, 2, 2]),
-                        op=ALU.mult,
-                    )
-
-        def x_quant(q):
-            nc.vector.quantize_mx(
-                out=xq_c[q][:].rearrange("p i g r -> p (i g r)").bitcast(FP8X4),
-                scales=xq_s[q][:].rearrange("p i g r -> p (i g r)"),
-                in_=xg[q][:].rearrange("p i g r t -> p (i g r t)"),
+        def x_words_out(i):
+            xg[i] = work.tile([P, G, P, 4], BF16, name="xg", align_bytes=64, bufs=3)
+            nc.scalar.copy(
+                out=xg[i][:].rearrange("p g r t -> p (g r t)").bitcast(F32).rearrange("p (g r u) -> p g r u", g=G, u=2),
+                in_=xt[i][:].rearrange("p g u r -> p g r u"),
             )
 
-        scb, nmax, zs, et, p1n = {}, {}, {}, {}, {}
-
-        def scores(q):
-            scb[q] = psum.tile([P, 2, C], F32, name="mm", bufs=6)
-            for i in range(2):
-                for g in range(G):
-                    nc.tensor.matmul_mx(
-                        out=scb[q][:, i, :],
-                        lhsT=xq_c[q][:, i, g, :].bitcast(FP8X4),
-                        lhsT_scale=xq_s[q][:, i, g, :],
-                        rhs=wk_c[:, g, :].bitcast(FP8X4),
-                        rhs_scale=wk_s[:, g, :],
-                        start=(g == 0),
-                        stop=(g == G - 1),
-                    )
-
-        def soft_max(q):
-            mx = work.tile([P, 16], F32, name="mx")
-            nc.vector.tensor_reduce(out=mx[:], in_=scb[q][:].rearrange("p i (k n) -> p (i k) n", n=N), axis=AX.X, op=ALU.max)
-            nmax[q] = work.tile([P, 16], F32, name="nmax")
-            nc.vector.tensor_scalar(out=nmax[q][:], in0=mx[:], scalar1=-1.0, scalar2=None, op0=ALU.mult)
-
-        def soft_exp(q):
-            et[q] = work.tile([P, 2, 2, H, N], F32, name="et", bufs=4)
-            zs[q] = work.tile([P, 2, 2, H], F32, name="zs", bufs=4)
-            for i in range(2):
-                for a in range(2):
-                    for h in range(H):
-                        k = a * H + h
-                        nc.scalar.activation(
-                            out=et[q][:, i, a, h, :],
-                            in_=scb[q][:, i, k * N : (k + 1) * N],
-                            func=ACT.Exp,
-                            bias=nmax[q][:, i * 8 + k : i * 8 + k + 1],
-                            accum_out=zs[q][:, i, a, h : h + 1],
-                        )
-
-        def soft_norm(q):
-            zz = work.tile([P, 2, H], F32, name="zz")
-            nc.vector.tensor_tensor(out=zz[:], in0=zs[q][:, :, 0, :], in1=zs[q][:, :, 1, :], op=ALU.mult)
-            rz = work.tile([P, 2, H], F32, name="rz")
-            nc.vector.reciprocal(out=rz[:], in_=zz[:])
-            p1n[q] = work.tile([P, 2, H, N], F32, name="p1n", bufs=4)
-            for i in range(2):
-                nc.vector.tensor_tensor(
-                    out=p1n[q][:, i], in0=et[q][:, i, 0], in1=rz[:, i, :].unsqueeze(2).to_broadcast([P, H, N]), op=ALU.mult
-                )
-
-        prod = {}
-
-        def products(i, which):
-            q, j = i // 2, i % 2
-            for h in range(H):
-                e = HEAD_ENGINE[h]
-                if e != which:
-                    continue
-                pt = work.tile([P, 4, N, 8], F32, name="prod%d" % h, align_bytes=64)
-                prod[i, h] = pt
-                if e == "S":
-                    src = et[q][:, j, 1, h, :].rearrange("p (m j) -> p m j", m=4)
-                    for k in range(N):
-                        nc.scalar.activation(out=pt[:, :, k, :], in_=src, func=ACT.Copy, scale=p1n[q][:, j, h, k : k + 1])
-                else:
-                    eng = nc.vector if e == "V" else nc.gpsimd
-                    eng.tensor_tensor(
-                        out=pt[:],
-                        in0=p1n[q][:, j, h, :].unsqueeze(1).unsqueeze(3).to_broadcast([P, 4, N, 8]),
-                        in1=et[q][:, j, 1, h, :].rearrange("p (m j) -> p m j", m=4).unsqueeze(2).to_broadcast([P, 4, N, 8]),
-                        op=ALU.mult,
-                    )
-
-        ut, ug = {}, {}
-
-        def u_transposes(i):
-            ut[i] = []
+        def x_transposes(i):
+            words = xw[i][:].bitcast(F32)
+            xt[i] = psum.tile([P, G, 2, P], F32, name="mm", bufs=4)
             for g in range(G):
-                bank = psum.tile([P, 4, P], F32, name="ut", bufs=2)
-                for m in range(4):
-                    for h in range(H):
-                        nc.tensor.matmul(
-                            out=bank[:, m, :],
-                            lhsT=prod[i, h][:, m, 16 * g : 16 * g + 16, :].rearrange("p i j -> p (i j)"),
-                            rhs=ident[:],
-                            is_transpose=True,
-                            start=(h == 0),
-                            stop=(h == H - 1),
-                        )
-                ut[i].append(bank)
+                for u in range(2):
+                    w0 = g * 256 + u
+                    nc.tensor.transpose(xt[i][:, g, u, :], words[:, w0 : w0 + 255 : 2], ident[:])
 
-        def u_empty(i):
-            ug[i] = work.tile([P, G, P, 4], BF16, name="ug", align_bytes=64)
+        def x_empty(i):
+            xg[i] = work.tile([P, G, P, 4], BF16, name="xg", align_bytes=64, bufs=3)
             for g in range(G):
                 nc.vector.tensor_tensor(
-                    out=ug[i][:, g],
-                    in0=ut[i][g][:].rearrange("p m r -> p r m"),
-                    in1=gain_t[:, g].unsqueeze(1).to_broadcast([P, P, 4]),
+                    out=xg[i][:, g].rearrange("p r (u e) -> p r u e", u=2),
+                    in0=xt[i][:, g].rearrange("p u r -> p (u r)").bitcast(BF16).rearrange("p (u r e) -> p r u e", u=2, e=2),
+                    in1=scale_t[:, g].rearrange("p (u e) -> p u e", u=2).unsqueeze(1).to_broadcast([P, P, 2, 2]),
                     op=ALU.mult,
                 )
 
-        def u_quant(i):
+        def quant(c, s, src):
             nc.vector.quantize_mx(
-                out=uq_c[i][:].rearrange("p g r -> p (g r)").bitcast(FP8X4),
-                scales=uq_s[i][:].rearrange("p g r -> p (g r)"),
-                in_=ug[i][:].rearrange("p g r t -> p (g r t)"),
+                out=c[:].rearrange("p g r -> p (g r)").bitcast(FP8X4),
+                scales=s[:].rearrange("p g r -> p (g r)"),
+                in_=src[:].rearrange("p g r t -> p (g r t)"),
             )
 
-        ab, mb, gate = {}, {}, {}
+        scb, nmax, zs, et, rzs, p1n, p2, p2s = {}, {}, {}, {}, {}, {}, {}, {}
+
+        def scores(i):
+            scb[i] = psum.tile([P, C], F32, name="mm", bufs=4)
+            for g in range(G):
+                nc.tensor.matmul_mx(
+                    out=scb[i][:],
+                    lhsT=xq_c[i][:, g, :].bitcast(FP8X4),
+                    lhsT_scale=xq_s[i][:, g, :],
+                    rhs=wk_c[:, g, :].bitcast(FP8X4),
+                    rhs_scale=wk_s[:, g, :],
+                    start=(g == 0),
+                    stop=(g == G - 1),
+                )
+
+        def soft_max(i):
+            nmax[i] = work.tile([P, 8], F32, name="nmax", bufs=8)
+            nc.vector.tensor_reduce(
+                out=nmax[i][:], in_=scb[i][:].rearrange("p (k n) -> p k n", n=N), axis=AX.X, op=ALU.max, negate=True
+            )
+
+        def soft_exp(i):
+            et[i] = work.tile([P, 2, H, N], F32, name="et", bufs=8)
+            zs[i] = work.tile([P, 2, H], F32, name="zs", bufs=8)
+            for a in range(2):
+                for h in range(H):
+                    k = a * H + h
+                    nc.scalar.activation(
+                        out=et[i][:, a, h, :],
+                        in_=scb[i][:, k * N : (k + 1) * N],
+                        func=ACT.Exp,
+                        bias=nmax[i][:, k : k + 1],
+                        accum_out=zs[i][:, a, h : h + 1],
+                    )
+
+        def norm_z(i):
+            rzs[i] = work.tile([P, 2, H], F32, name="rz", bufs=8)
+            nc.vector.tensor_tensor(out=rzs[i][:, 0], in0=zs[i][:, 0, :], in1=zs[i][:, 1, :], op=ALU.mult)
+
+        def norm_r(i):
+            nc.vector.reciprocal(out=rzs[i][:, 1], in_=rzs[i][:, 0])
+
+        def norm_m(i):
+            p1n[i] = work.tile([P, H, N], F32, name="p1n", bufs=8)
+            nc.vector.tensor_tensor(
+                out=p1n[i][:], in0=et[i][:, 0], in1=rzs[i][:, 1].unsqueeze(2).to_broadcast([P, H, N]), op=ALU.mult
+            )
+
+        def p2_t(i):
+            p2[i] = psum.tile([P, 2, P], F32, name="p2", bufs=2)
+            nc.tensor.transpose(p2[i][:, 0, :], et[i][:, 1].rearrange("p h n -> p (h n)"), ident[:])
+
+        def p2_c(i):
+            p2s[i] = work.tile([P, P], F32, name="p2s", bufs=4)
+            nc.scalar.copy(out=p2s[i][:], in_=p2[i][:, 0, :])
+
+        def p2_b(i):
+            nc.tensor.transpose(p2[i][:, 1, :], p2s[i][:], ident[:])
+
+        prod = {}
+
+        def products(i, g, h, which):
+            if (i, h) not in prod:
+                prod[i, h] = work.tile([P, G, 4, 16, 8], F32, name="prod%d" % h, align_bytes=64, bufs=3)
+            k0, k1 = 16 * g, 16 * g + 16
+            pt = prod[i, h]
+            src = et[i][:, 1, h, :]
+            if which == "V" and P2:
+                src = p2[i][:, 1, h * N : h * N + N]
+            src = src.rearrange("p (m j) -> p m j", m=4)
+            if which == "S":
+                for k in range(k0, k1):
+                    nc.scalar.activation(out=pt[:, g, :, k - k0, :], in_=src, func=ACT.Copy, scale=p1n[i][:, h, k : k + 1])
+            else:
+                eng = nc.vector if which == "V" else nc.gpsimd
+                eng.tensor_tensor(
+                    out=pt[:, g],
+                    in0=p1n[i][:, h, k0:k1].unsqueeze(1).unsqueeze(3).to_broadcast([P, 4, 16, 8]),
+                    in1=src.unsqueeze(2).to_broadcast([P, 4, 16, 8]),
+                    op=ALU.mult,
+                )
+
+        ut, ug = {}, {}
+
+        def u_transposes(i, g):
+            ut[i, g] = psum.tile([P, 4, P], F32, name="ut", bufs=2)
+            for m in range(4):
+                for h in range(H):
+                    nc.tensor.matmul(
+                        out=ut[i, g][:, m, :],
+                        lhsT=prod[i, h][:, g, m].rearrange("p i j -> p (i j)"),
+                        rhs=ident[:],
+                        is_transpose=True,
+                        start=(h == 0),
+                        stop=(h == H - 1),
+                    )
+
+        def u_empty(i, g):
+            if i not in ug:
+                ug[i] = work.tile([P, G, P, 4], BF16, name="ug", align_bytes=64, bufs=3)
+            nc.vector.tensor_tensor(
+                out=ug[i][:, g],
+                in0=ut[i, g][:].rearrange("p m r -> p r m"),
+                in1=gain_t[:, g].unsqueeze(1).to_broadcast([P, P, 4]),
+                op=ALU.mult,
+            )
+
+        ab, mb, gate, ot = {}, {}, {}, {}
 
         def mm(lc, ls, nm, nh):
-            bank = psum.tile([P, 512], F32, name="mm", bufs=6)
+            bank = psum.tile([P, 512], F32, name="mm", bufs=4)
             for g in range(G):
                 nc.tensor.matmul_mx(
                     out=bank[:],
-                    lhsT=lc[g].bitcast(FP8X4),
-                    lhsT_scale=ls[g],
+                    lhsT=lc[:, g, :].bitcast(FP8X4),
+                    lhsT_scale=ls[:, g, :],
                     rhs=codes[nm][0][g][nh][:].bitcast(FP8X4),
                     rhs_scale=codes[nm][1][g][nh][:],
                     start=(g == 0),
@@ -274,97 +316,75 @@ def tile_productkeysoftmemoryplus_kernel(tc, x_bytes, x_scale, wk, slot_gain, va
                 )
             return bank
 
-        def a_mm(i):
-            q, j = i // 2, i % 2
-            for nh in range(2):
-                ab[i, nh] = mm([xq_c[q][:, j, g, :] for g in range(G)], [xq_s[q][:, j, g, :] for g in range(G)], "wg", nh)
+        def silu(i, nh):
+            gate[i, nh] = work.tile([P, 512], F32, name="gate", bufs=8)
+            nc.scalar.activation(out=gate[i, nh][:], in_=ab[i, nh][:], func=ACT.Silu)
 
-        def m_mm(i):
-            for nh in range(2):
-                mb[i, nh] = mm([uq_c[i][:, g, :] for g in range(G)], [uq_s[i][:, g, :] for g in range(G)], "val", nh)
+        def final(i, nh):
+            ot[i, nh] = work.tile([P, 512], F32, name="o", bufs=6)
+            nc.vector.tensor_tensor(out=ot[i, nh][:], in0=mb[i, nh][:], in1=gate[i, nh][:], op=ALU.mult)
+            nc.sync.dma_start(out=out[i * P : (i + 1) * P, nh * 512 : (nh + 1) * 512], in_=ot[i, nh][:])
 
-        def silu(i):
-            gate[i] = work.tile([P, 2, 512], F32, name="gate")
-            for nh in range(2):
-                nc.scalar.activation(out=gate[i][:, nh, :], in_=ab[i, nh][:], func=ACT.Silu)
+        def run(tok):
+            op, args = tok.split(":")[0], [v if v in "VSG" else int(v) for v in tok.split(":")[1:]]
+            if op == "WK":
+                prep_wk_i()
+            elif op == "WKQ":
+                prep_wk_q()
+            elif op == "WD":
+                widen(*args)
+            elif op == "XT":
+                x_transposes(*args)
+            elif op == "XP":
+                x_scale_product(*args)
+            elif op == "XE":
+                x_words_out(*args) if II else x_empty(*args)
+            elif op == "XQ":
+                quant(xq_c[args[0]], xq_s[args[0]], xg[args[0]])
+            elif op == "SC":
+                scores(*args)
+            elif op == "MX":
+                soft_max(*args)
+            elif op == "EX":
+                soft_exp(*args)
+            elif op == "NZ":
+                norm_z(*args)
+            elif op == "NR":
+                norm_r(*args)
+            elif op == "NM":
+                norm_m(*args)
+            elif op == "PT":
+                p2_t(*args)
+            elif op == "PC":
+                p2_c(*args)
+            elif op == "PB":
+                p2_b(*args)
+            elif op == "PR":
+                products(*args)
+            elif op == "UT":
+                u_transposes(*args)
+            elif op == "UE":
+                u_empty(*args)
+            elif op == "UQ":
+                quant(uq_c[args[0]], uq_s[args[0]], ug[args[0]])
+            elif op == "A":
+                ab[args[0], args[1]] = mm(xq_c[args[0]], xq_s[args[0]], "wg", args[1])
+            elif op == "SL":
+                silu(*args)
+            elif op == "MM":
+                mb[args[0], args[1]] = mm(uq_c[args[0]], uq_s[args[0]], "val", args[1])
+            elif op == "FN":
+                final(*args)
+            elif op == "WI":
+                wi(*args)
+            elif op == "WQ":
+                wq(*args)
+            else:
+                raise ValueError(op)
 
-        def final(i):
-            o = work.tile([P, 2, 512], F32, name="o", bufs=3)
-            for nh in range(2):
-                nc.vector.tensor_tensor(out=o[:, nh, :], in0=mb[i, nh][:], in1=gate[i][:, nh, :], op=ALU.mult)
-            nc.sync.dma_start(out=out[i * P : (i + 1) * P, :], in_=o[:].rearrange("p a n -> p (a n)"))
-
-        def front(q):
-            x_transposes(q)
-            x_empty(q)
-            x_quant(q)
-            scores(q)
-            soft_max(q)
-            soft_exp(q)
-            soft_norm(q)
-
-        def prods(i):
-            products(i, "S")
-            products(i, "G")
-            products(i, "V")
-
-        def mid(i):
-            u_transposes(i)
-            u_empty(i)
-            u_quant(i)
-
-        def back(i):
-            a_mm(i)
-            silu(i)
-            m_mm(i)
-            final(i)
-
-        wjobs = [("wg", wg_raw, g, nh, WG_ENGINE[2 * g + nh]) for g in range(G) for nh in range(2)]
-        wjobs += [("val", val_raw, g, nh, VAL_ENGINE[2 * g + nh]) for g in range(G) for nh in range(2)]
-
-        def wprep(j):
-            nm, raw, g, nh, eng = wjobs[j]
-            interleave_w(nm, raw, g, nh, eng)
-            quant_w(nm, g, nh)
-
-        widen(0, "S")
-        prep_wk()
-        front(0)
-        widen(1, "G")
-        wprep(0)
-        wprep(1)
-        prods(0)
-        front(1)
-        widen(2, "G")
-        mid(0)
-        prods(1)
-        wprep(2)
-        wprep(3)
-        front(2)
-        widen(3, "G")
-        mid(1)
-        prods(2)
-        wprep(4)
-        wprep(5)
-        front(3)
-        mid(2)
-        prods(3)
-        wprep(6)
-        wprep(7)
-        back(0)
-        mid(3)
-        prods(4)
-        back(1)
-        back(2)
-        mid(4)
-        prods(5)
-        back(3)
-        mid(5)
-        prods(6)
-        back(4)
-        mid(6)
-        prods(7)
-        back(5)
-        mid(7)
-        back(6)
-        back(7)
+        with tc.manual_schedule():
+            warm = work.tile([P, 1], F32, name="warm")
+            nc.vector.memset(warm[:], 0.0)
+            nc.scalar.activation(out=warm[:], in_=warm[:], func=ACT.Exp)
+            for tok in PLAN.split():
+                run(tok)

from contextlib import ExitStack

import concourse.mybir as mybir
from concourse.masks import make_identity

T, D, C, SLOTS = 1024, 1024, 256, 1024
H, N = 4, 32
P = 128
G = 2
TILES = T // P
PAIRS = TILES // 2

FLOPS = 2 * T * D * (C + D + D)

F32 = mybir.dt.float32
BF16 = mybir.dt.bfloat16
U32 = mybir.dt.uint32
U8 = mybir.dt.uint8
FP8 = mybir.dt.float8_e4m3fn
FP8X4 = mybir.dt.float8_e4m3fn_x4
ACT = mybir.ActivationFunctionType
ALU = mybir.AluOpType
AX = mybir.AxisListType

PLAN = """ WD:0:V XT:0 WK WD:1:S XT:1 WKQ XE:0 WI:0:G:384:512 WD:2:S WI:0:G:256:384 XE:1 WD:3:S XT:2 WI:0:G:128:256 XQ:0
 XT:3 XE:2 WI:0:G:0:128 WD:4:S WI:1:G:384:512 XE:3 WI:1:G:256:384 WD:5:S XT:4 SC:0 XQ:1 XE:4 WI:1:G:128:256
 WD:6:S XT:5 WI:1:G:0:128 SC:1 MX:0 WD:7:S XQ:2 XE:5 EX:0 MX:1 WI:2:V:256:512 WI:3:S:256:512 PT:0 XT:6 NZ:0
 SC:2 NR:0 WI:2:V:0:256 EX:1 NM:0 XQ:3 PR:0:0:3:G XE:6 WI:3:S:0:256 PT:1 XT:7 SC:3 MX:2 WI:4:S:256:512 NZ:1
 XQ:4 NR:1 MX:3 SC:4 XQ:5 NM:1 PC:1 XQ:6 PC:0 PB:1 WI:4:S:0:256 PR:1:0:0:G MX:4 PB:0 PR:1:0:1:V PR:1:0:3:V
 PR:1:0:2:G EX:2 PR:1:1:1:V PR:0:0:0:V WI:5:S:256:512 PT:2 PR:1:1:0:G PR:0:0:1:V PR:0:0:2:V PC:2 WI:6:S:256:512
 PR:1:1:2:G PR:0:1:0:V UT:0:0 PR:0:1:1:V PR:0:1:2:V PR:1:1:3:G WI:5:S:0:256 PR:0:1:3:V UT:0:1 NZ:2 XE:7
 WI:7:G:384:512 EX:3 WI:7:G:256:384 WI:6:S:0:256 NR:2 PB:2 SC:5 XQ:7 PT:3 UE:0:0 WI:7:G:128:256 PC:3 UE:0:1
 PB:3 UT:1:0 MX:5 NZ:3 NM:2 PR:2:0:0:S PR:2:0:1:G PR:2:0:2:V SC:6 UT:1:1 PR:2:0:3:V PR:2:1:1:S PR:2:1:2:G
 PR:2:1:0:V PR:2:1:3:S UE:1:0 SC:7 WI:7:G:0:128 MX:6 UE:1:1 EX:4 WQ:1 PT:4 WQ:2 UT:2:0 PC:4 EX:5 WQ:0 MX:7 EX:6
 A:0:0 WQ:3 NZ:4 PB:4 NR:3 WQ:4 EX:7 UT:2:1 WQ:5 SL:0:0 NZ:5 NM:3 A:1:0 PR:3:0:1:G PR:3:0:0:V A:0:1 PR:3:0:2:V
 A:2:0 PR:3:0:3:G PR:3:1:1:V SL:0:1 PR:3:1:2:V A:1:1 SL:1:0 PR:3:1:0:G PR:3:1:3:V A:3:0 SL:1:1 UE:2:0 A:2:1
 SL:2:0 WQ:6 UT:3:0 SL:3:0 UE:2:1 SL:2:1 NZ:6 NZ:7 WQ:7 UT:3:1 NR:4 UQ:0 NM:4 PR:4:0:0:G PR:4:0:3:S PR:4:0:2:V
 MM:0:0 PR:4:1:0:V PR:4:1:1:S MM:0:1 PR:4:0:1:G PR:4:1:3:V A:4:0 PR:4:1:2:S FN:0:0 A:3:1 FN:0:1 A:4:1 SL:4:0
 UQ:1 A:5:0 UE:3:0 SL:3:1 MM:1:0 UE:3:1 SL:4:1 MM:1:1 FN:1:0 UT:4:0 NR:5 SL:5:0 NM:5 UQ:2 PR:5:0:0:S PR:5:0:1:G
 FN:1:1 UT:4:1 PR:5:0:3:S UQ:3 PR:5:0:2:G NR:6 PR:5:1:1:S MM:2:0 MM:2:1 PR:5:1:2:S NM:6 PR:5:1:0:G FN:2:0 A:5:1
 NR:7 A:6:0 SL:5:1 NM:7 MM:3:0 PR:5:1:3:G FN:2:1 SL:6:0 MM:3:1 UE:4:0 PR:6:0:1:S A:6:1 UE:4:1 PR:6:0:0:G
 PR:6:0:3:S UT:5:0 UQ:4 PR:6:1:0:S PR:6:0:2:G FN:3:0 UT:5:1 FN:3:1 PR:6:1:2:S UE:5:0 PR:6:1:1:G PR:6:1:3:S
 A:7:0 UE:5:1 MM:4:0 PR:7:0:0:G SL:6:1 MM:4:1 PR:7:0:1:S A:7:1 UQ:5 PR:7:0:3:G FN:4:0 UT:6:0 PR:7:0:2:S FN:4:1
 PR:7:1:1:S PR:7:1:0:G UT:6:1 UE:6:0 PR:7:1:3:S PR:7:1:2:G SL:7:0 MM:5:0 UE:6:1 SL:7:1 MM:5:1 UQ:6 UT:7:0
 FN:5:0 FN:5:1 UT:7:1 UE:7:0 MM:6:0 UE:7:1 MM:6:1 UQ:7 FN:6:0 MM:7:0 FN:6:1 MM:7:1 FN:7:0 FN:7:1"""
P2 = True
II = False


def tile_productkeysoftmemoryplus_kernel(tc, x_bytes, x_scale, wk, slot_gain, values, wg, out):
    nc = tc.nc
    with ExitStack() as ctx:
        keep = ctx.enter_context(tc.tile_pool(name="keep", bufs=1))
        work = ctx.enter_context(tc.tile_pool(name="work", bufs=2))
        psum = ctx.enter_context(tc.psum_pool(name="psum", bufs=1))

        ident = keep.tile([P, P], F32, name="ident")
        xb = [keep.tile([P, D], U8, name="xb%d" % i) for i in range(TILES)]
        scale_t = keep.tile([P, G, 4], F32, name="scale_t")
        scale_b = keep.tile([P, D], F32, name="scale_b")
        gain_t = keep.tile([P, G, 4], BF16, name="gain_t")
        wk_raw = keep.tile([P, G, 4, C], BF16, name="wk_raw")
        wg_raw = [keep.tile([P, 4, D], BF16, name="wg_raw%d" % g) for g in range(G)]
        val_raw = [keep.tile([P, 4, D], BF16, name="val_raw%d" % g) for g in range(G)]

        def load_x(i):
            nc.sync.dma_start(out=xb[i][:], in_=x_bytes[i * P : (i + 1) * P, :])

        def load_w(dst, src, g):
            nc.sync.dma_start(out=dst[g][:], in_=src[g * 512 : (g + 1) * 512, :].rearrange("(p t) n -> p t n", t=4))

        load_x(0)
        if II:
            nc.sync.dma_start(out=scale_b[:], in_=x_scale.rearrange("o k -> (o k)").partition_broadcast(P))
        else:
            nc.sync.dma_start(out=scale_t[:], in_=x_scale.rearrange("o (g p t) -> p (o g) t", p=P, t=4))
        nc.sync.dma_start(out=wk_raw[:], in_=wk.rearrange("(g p t) c -> p g t c", p=P, t=4))
        load_x(1)
        load_w(wg_raw, wg, 0)
        nc.sync.dma_start(out=gain_t[:], in_=slot_gain.rearrange("(g p t) -> p g t", p=P, t=4))
        load_x(2)
        load_x(3)
        load_w(wg_raw, wg, 1)
        for i in range(4, TILES):
            load_x(i)
        load_w(val_raw, values, 0)
        load_w(val_raw, values, 1)

        make_identity(nc, ident[:])

        wk_i = keep.tile([P, G, C, 4], BF16, name="wk_i", align_bytes=64)
        wk_c = keep.tile([P, G, C], U32, name="wk_c", align_bytes=64)
        wk_s = keep.tile([P, G, C], U8, name="wk_s", align_bytes=64)

        def prep_wk_i():
            for g in range(G):
                src = wk_raw[:, g].rearrange("p t (h a n) -> p t h a n", h=H, a=2)
                nc.vector.tensor_copy(
                    out=wk_i[:, g, 0:128, :].rearrange("p (h n) t -> p h n t", h=H),
                    in_=src[:, :, :, 0, :].rearrange("p t h n -> p h n t"),
                )
                for h in range(H):
                    nc.vector.tensor_copy(
                        out=wk_i[:, g, 128 + 32 * h : 160 + 32 * h, :].rearrange("p (m j) t -> p m j t", m=4),
                        in_=src[:, :, h, 1, :].rearrange("p t (j m) -> p m j t", m=4),
                    )

        def prep_wk_q():
            nc.vector.quantize_mx(
                out=wk_c[:].rearrange("p g c -> p (g c)").bitcast(FP8X4),
                scales=wk_s[:].rearrange("p g c -> p (g c)"),
                in_=wk_i[:].rearrange("p g c t -> p (g c t)"),
            )

        codes = {}
        for nm in ("wg", "val"):
            codes[nm] = (
                [[keep.tile([P, 512], U32, name="%s_c%d%d" % (nm, g, nh), align_bytes=64) for nh in range(2)] for g in range(G)],
                [[keep.tile([P, 512], U8, name="%s_s%d%d" % (nm, g, nh), align_bytes=64) for nh in range(2)] for g in range(G)],
            )
        staged = {}

        def wi(j, eng, c0, c1):
            nm, raw, g, nh = (("wg", wg_raw), ("val", val_raw))[j // 4] + ((j // 2) % 2, j % 2)
            if j not in staged:
                staged[j] = work.tile([P, 512, 4], BF16, name="w_i", align_bytes=64, bufs=8)
            st = staged[j][:, c0:c1, :]
            src = raw[g][:, :, nh * 512 + c0 : nh * 512 + c1].rearrange("p t n -> p n t")
            if eng == "V":
                nc.vector.tensor_copy(out=st, in_=src)
            elif eng == "S":
                nc.scalar.copy(out=st, in_=src)
            else:
                nc.gpsimd.tensor_scalar(out=st, in0=src, scalar1=1.0, scalar2=0.0, op0=ALU.mult, op1=ALU.add)

        def wq(j):
            nm, g, nh = ("wg", "val")[j // 4], (j // 2) % 2, j % 2
            nc.vector.quantize_mx(
                out=codes[nm][0][g][nh][:].bitcast(FP8X4),
                scales=codes[nm][1][g][nh][:],
                in_=staged[j][:].rearrange("p n t -> p (n t)"),
            )

        xw, xt, xg = {}, {}, {}
        xq_c = [keep.tile([P, G, P], U32, name="xq_c%d" % i, align_bytes=64) for i in range(TILES)]
        xq_s = [keep.tile([P, G, P], U8, name="xq_s%d" % i, align_bytes=64) for i in range(TILES)]
        uq_c = [keep.tile([P, G, P], U32, name="uq_c%d" % i, align_bytes=64) for i in range(TILES)]
        uq_s = [keep.tile([P, G, P], U8, name="uq_s%d" % i, align_bytes=64) for i in range(TILES)]

        def widen(i, e):
            xw[i] = work.tile([P, D], BF16, name="xw", align_bytes=64, bufs=3)
            src = xb[i][:].bitcast(FP8)
            if e == "S":
                nc.scalar.copy(out=xw[i][:], in_=src)
            elif e == "V":
                nc.vector.tensor_copy(out=xw[i][:], in_=src)
            else:
                nc.gpsimd.tensor_copy(out=xw[i][:], in_=src)

        def x_scale_product(i):
            xw[i] = work.tile([P, D], BF16, name="xw", align_bytes=64, bufs=3)
            nc.vector.tensor_tensor(out=xw[i][:], in0=xb[i][:].bitcast(FP8), in1=scale_b[:], op=ALU.mult)

        def x_words_out(i):
            xg[i] = work.tile([P, G, P, 4], BF16, name="xg", align_bytes=64, bufs=3)
            nc.scalar.copy(
                out=xg[i][:].rearrange("p g r t -> p (g r t)").bitcast(F32).rearrange("p (g r u) -> p g r u", g=G, u=2),
                in_=xt[i][:].rearrange("p g u r -> p g r u"),
            )

        def x_transposes(i):
            words = xw[i][:].bitcast(F32)
            xt[i] = psum.tile([P, G, 2, P], F32, name="mm", bufs=4)
            for g in range(G):
                for u in range(2):
                    w0 = g * 256 + u
                    nc.tensor.transpose(xt[i][:, g, u, :], words[:, w0 : w0 + 255 : 2], ident[:])

        def x_empty(i):
            xg[i] = work.tile([P, G, P, 4], BF16, name="xg", align_bytes=64, bufs=3)
            for g in range(G):
                nc.vector.tensor_tensor(
                    out=xg[i][:, g].rearrange("p r (u e) -> p r u e", u=2),
                    in0=xt[i][:, g].rearrange("p u r -> p (u r)").bitcast(BF16).rearrange("p (u r e) -> p r u e", u=2, e=2),
                    in1=scale_t[:, g].rearrange("p (u e) -> p u e", u=2).unsqueeze(1).to_broadcast([P, P, 2, 2]),
                    op=ALU.mult,
                )

        def quant(c, s, src):
            nc.vector.quantize_mx(
                out=c[:].rearrange("p g r -> p (g r)").bitcast(FP8X4),
                scales=s[:].rearrange("p g r -> p (g r)"),
                in_=src[:].rearrange("p g r t -> p (g r t)"),
            )

        scb, nmax, zs, et, rzs, p1n, p2, p2s = {}, {}, {}, {}, {}, {}, {}, {}

        def scores(i):
            scb[i] = psum.tile([P, C], F32, name="mm", bufs=4)
            for g in range(G):
                nc.tensor.matmul_mx(
                    out=scb[i][:],
                    lhsT=xq_c[i][:, g, :].bitcast(FP8X4),
                    lhsT_scale=xq_s[i][:, g, :],
                    rhs=wk_c[:, g, :].bitcast(FP8X4),
                    rhs_scale=wk_s[:, g, :],
                    start=(g == 0),
                    stop=(g == G - 1),
                )

        def soft_max(i):
            nmax[i] = work.tile([P, 8], F32, name="nmax", bufs=8)
            nc.vector.tensor_reduce(
                out=nmax[i][:], in_=scb[i][:].rearrange("p (k n) -> p k n", n=N), axis=AX.X, op=ALU.max, negate=True
            )

        def soft_exp(i):
            et[i] = work.tile([P, 2, H, N], F32, name="et", bufs=8)
            zs[i] = work.tile([P, 2, H], F32, name="zs", bufs=8)
            for a in range(2):
                for h in range(H):
                    k = a * H + h
                    nc.scalar.activation(
                        out=et[i][:, a, h, :],
                        in_=scb[i][:, k * N : (k + 1) * N],
                        func=ACT.Exp,
                        bias=nmax[i][:, k : k + 1],
                        accum_out=zs[i][:, a, h : h + 1],
                    )

        def norm_z(i):
            rzs[i] = work.tile([P, 2, H], F32, name="rz", bufs=8)
            nc.vector.tensor_tensor(out=rzs[i][:, 0], in0=zs[i][:, 0, :], in1=zs[i][:, 1, :], op=ALU.mult)

        def norm_r(i):
            nc.vector.reciprocal(out=rzs[i][:, 1], in_=rzs[i][:, 0])

        def norm_m(i):
            p1n[i] = work.tile([P, H, N], F32, name="p1n", bufs=8)
            nc.vector.tensor_tensor(
                out=p1n[i][:], in0=et[i][:, 0], in1=rzs[i][:, 1].unsqueeze(2).to_broadcast([P, H, N]), op=ALU.mult
            )

        def p2_t(i):
            p2[i] = psum.tile([P, 2, P], F32, name="p2", bufs=2)
            nc.tensor.transpose(p2[i][:, 0, :], et[i][:, 1].rearrange("p h n -> p (h n)"), ident[:])

        def p2_c(i):
            p2s[i] = work.tile([P, P], F32, name="p2s", bufs=4)
            nc.scalar.copy(out=p2s[i][:], in_=p2[i][:, 0, :])

        def p2_b(i):
            nc.tensor.transpose(p2[i][:, 1, :], p2s[i][:], ident[:])

        prod = {}

        def products(i, g, h, which):
            if (i, h) not in prod:
                prod[i, h] = work.tile([P, G, 4, 16, 8], F32, name="prod%d" % h, align_bytes=64, bufs=3)
            k0, k1 = 16 * g, 16 * g + 16
            pt = prod[i, h]
            src = et[i][:, 1, h, :]
            if which == "V" and P2:
                src = p2[i][:, 1, h * N : h * N + N]
            src = src.rearrange("p (m j) -> p m j", m=4)
            if which == "S":
                for k in range(k0, k1):
                    nc.scalar.activation(out=pt[:, g, :, k - k0, :], in_=src, func=ACT.Copy, scale=p1n[i][:, h, k : k + 1])
            else:
                eng = nc.vector if which == "V" else nc.gpsimd
                eng.tensor_tensor(
                    out=pt[:, g],
                    in0=p1n[i][:, h, k0:k1].unsqueeze(1).unsqueeze(3).to_broadcast([P, 4, 16, 8]),
                    in1=src.unsqueeze(2).to_broadcast([P, 4, 16, 8]),
                    op=ALU.mult,
                )

        ut, ug = {}, {}

        def u_transposes(i, g):
            ut[i, g] = psum.tile([P, 4, P], F32, name="ut", bufs=2)
            for m in range(4):
                for h in range(H):
                    nc.tensor.matmul(
                        out=ut[i, g][:, m, :],
                        lhsT=prod[i, h][:, g, m].rearrange("p i j -> p (i j)"),
                        rhs=ident[:],
                        is_transpose=True,
                        start=(h == 0),
                        stop=(h == H - 1),
                    )

        def u_empty(i, g):
            if i not in ug:
                ug[i] = work.tile([P, G, P, 4], BF16, name="ug", align_bytes=64, bufs=3)
            nc.vector.tensor_tensor(
                out=ug[i][:, g],
                in0=ut[i, g][:].rearrange("p m r -> p r m"),
                in1=gain_t[:, g].unsqueeze(1).to_broadcast([P, P, 4]),
                op=ALU.mult,
            )

        ab, mb, gate, ot = {}, {}, {}, {}

        def mm(lc, ls, nm, nh):
            bank = psum.tile([P, 512], F32, name="mm", bufs=4)
            for g in range(G):
                nc.tensor.matmul_mx(
                    out=bank[:],
                    lhsT=lc[:, g, :].bitcast(FP8X4),
                    lhsT_scale=ls[:, g, :],
                    rhs=codes[nm][0][g][nh][:].bitcast(FP8X4),
                    rhs_scale=codes[nm][1][g][nh][:],
                    start=(g == 0),
                    stop=(g == G - 1),
                )
            return bank

        def silu(i, nh):
            gate[i, nh] = work.tile([P, 512], F32, name="gate", bufs=8)
            nc.scalar.activation(out=gate[i, nh][:], in_=ab[i, nh][:], func=ACT.Silu)

        def final(i, nh):
            ot[i, nh] = work.tile([P, 512], F32, name="o", bufs=6)
            nc.vector.tensor_tensor(out=ot[i, nh][:], in0=mb[i, nh][:], in1=gate[i, nh][:], op=ALU.mult)
            nc.sync.dma_start(out=out[i * P : (i + 1) * P, nh * 512 : (nh + 1) * 512], in_=ot[i, nh][:])

        def run(tok):
            op, args = tok.split(":")[0], [v if v in "VSG" else int(v) for v in tok.split(":")[1:]]
            if op == "WK":
                prep_wk_i()
            elif op == "WKQ":
                prep_wk_q()
            elif op == "WD":
                widen(*args)
            elif op == "XT":
                x_transposes(*args)
            elif op == "XP":
                x_scale_product(*args)
            elif op == "XE":
                x_words_out(*args) if II else x_empty(*args)
            elif op == "XQ":
                quant(xq_c[args[0]], xq_s[args[0]], xg[args[0]])
            elif op == "SC":
                scores(*args)
            elif op == "MX":
                soft_max(*args)
            elif op == "EX":
                soft_exp(*args)
            elif op == "NZ":
                norm_z(*args)
            elif op == "NR":
                norm_r(*args)
            elif op == "NM":
                norm_m(*args)
            elif op == "PT":
                p2_t(*args)
            elif op == "PC":
                p2_c(*args)
            elif op == "PB":
                p2_b(*args)
            elif op == "PR":
                products(*args)
            elif op == "UT":
                u_transposes(*args)
            elif op == "UE":
                u_empty(*args)
            elif op == "UQ":
                quant(uq_c[args[0]], uq_s[args[0]], ug[args[0]])
            elif op == "A":
                ab[args[0], args[1]] = mm(xq_c[args[0]], xq_s[args[0]], "wg", args[1])
            elif op == "SL":
                silu(*args)
            elif op == "MM":
                mb[args[0], args[1]] = mm(uq_c[args[0]], uq_s[args[0]], "val", args[1])
            elif op == "FN":
                final(*args)
            elif op == "WI":
                wi(*args)
            elif op == "WQ":
                wq(*args)
            else:
                raise ValueError(op)

        with tc.manual_schedule():
            warm = work.tile([P, 1], F32, name="warm")
            nc.vector.memset(warm[:], 0.0)
            nc.scalar.activation(out=warm[:], in_=warm[:], func=ACT.Exp)
            for tok in PLAN.split():
                run(tok)
